import numpy as np
import ml_dtypes


def mxq(x, axis, fmt="e4m3"):
    dtype, down = {"e4m3": (ml_dtypes.float8_e4m3fn, 7), "e5m2": (ml_dtypes.float8_e5m2, 14)}[fmt]
    v = np.moveaxis(np.asarray(x, np.float32).astype(ml_dtypes.bfloat16).astype(np.float64), axis, -1)
    blocks = v.reshape(v.shape[:-1] + (-1, 32))
    amax = np.abs(blocks).max(-1, keepdims=True)
    byte = np.maximum(np.where(amax > 0, np.frexp(amax)[1] - 1 + 127, 0) - down, 1)
    scale = np.exp2(byte - 127.0)
    codes = (blocks / scale).astype(np.float32).astype(dtype).astype(np.float64)
    return np.moveaxis((codes * scale).reshape(v.shape), -1, axis)


WIDE = False


def mx_kscale(k):
    if not WIDE:
        return np.ones(k)
    levels = np.array([10, -10, 5, -5, 0])
    if k % 512:
        return np.exp2(np.random.permutation(np.resize(levels, k // 32))).repeat(32)
    a = np.empty((k // 512, 16))
    for p in range(k // 512):
        a[p, :8] = np.random.permutation(np.resize(levels, 8))
        for g in range(8):
            far = levels[np.abs(levels - a[p, g]) >= 10]
            a[p, g + 8] = far[np.random.randint(len(far))]
    return np.exp2(a.ravel()).repeat(32)


BF16 = ml_dtypes.bfloat16


def bf(x):
    return np.asarray(x, np.float32).astype(BF16)


def f64(x):
    return np.asarray(x).astype(np.float64)

def planes(Y):
    n, m = Y.shape
    b = f64(bf(Y)).reshape(n // 32, 32, m)
    amax = np.abs(b).max(1)
    byte = np.clip(np.where(amax > 0, np.frexp(amax)[1] - 1 + 127 - 7, 1), 1, 254)
    codes = (b * np.exp2(127.0 - byte)[:, None, :]).reshape(n, m).astype(np.float32).astype(ml_dtypes.float8_e4m3fn).view(np.uint8)
    words = codes.reshape(n // 512, 128, 4, m).transpose(0, 1, 3, 2)
    return np.ascontiguousarray(words), np.ascontiguousarray(byte.astype(np.uint8).reshape(n // 512, 16, m))


S, C, H, Q = 2048, 512, 8, 256

def sigmoid(x):
    return 1.0 / (1.0 + np.exp(-x))

def setup_inputs():
    s = mx_kscale(S)
    logits = 2.0 * np.random.randn(H, Q, S)
    e = np.exp(logits - logits.max(axis=-1, keepdims=True))
    probs = e / e.sum(axis=-1, keepdims=True)
    size = 2.0 * np.exp(0.8 * np.random.randn(C))
    mean = 0.3 * np.random.randn(C)
    values = size * (mean + np.random.randn(S, C))
    return {
        "attn": bf(probs * s),
        "values": bf(values / s[:, None]),
        "gate": bf(np.random.randn(C, H, Q)),
        "gate_bias": bf(0.5 * np.random.randn(C, H)),
    }

def reference(attn, values, gate, gate_bias):
    a = mxq(f64(attn).reshape(H * Q, S), 1, "e4m3")
    v = mxq(f64(values), 0, "e4m3")
    o = (v.T @ a.T).reshape(C, H, Q)
    y = sigmoid(f64(gate) + f64(gate_bias)[:, :, None]) * o
    Y = y.reshape(C, H * Q)
    words, scales = planes(Y)
    return y, words, scales

@@ -1,0 +1,273 @@
+from contextlib import ExitStack
+
+import concourse.mybir as mybir
+from concourse.masks import make_identity
+
+S, C, H, Q = 2048, 512, 8, 256
+FLOPS = 2 * C * H * Q * S
+
+F32 = mybir.dt.float32
+BF16 = mybir.dt.bfloat16
+I32 = mybir.dt.int32
+U32 = mybir.dt.uint32
+U8 = mybir.dt.uint8
+FP8X4 = mybir.dt.float8_e4m3fn_x4
+SIGMOID = mybir.ActivationFunctionType.Sigmoid
+MULT = mybir.AluOpType.mult
+
+P = 128
+PACK = 4
+K_PASS = P * PACK
+PASSES = S // K_PASS
+ROW_TILES = Q // P
+BANK = 512
+STAGED = 8
+SCALAR_SHARE = (32, 32, 0, 32)
+
+
+def tile_gated_cached_value_mix_g2_kernel(tc, attn, values, gate, gate_bias, out_0, out_1, out_2):
+    nc = tc.nc
+    with ExitStack() as ctx:
+        sb = ctx.enter_context(tc.tile_pool(name="sb", bufs=1))
+        ps = ctx.enter_context(tc.psum_pool(name="ps", bufs=1))
+        ctx.enter_context(tc.manual_schedule())
+
+        def tiles(pool, name, count, shape, dtype):
+            if pool is ps:
+                return [pool.tile(shape, dtype, name="%s%d" % (name, i)) for i in range(count)]
+            return [pool.tile(shape, dtype, name="%s%d" % (name, i), align_bytes=256) for i in range(count)]
+
+        ident = sb.tile([P, P], F32, name="ident", align_bytes=256)
+        bias = sb.tile([P, PACK * H], BF16, name="bias", align_bytes=256)
+        warm_in = sb.tile([P, 1], F32, name="warm_in")
+        warm_out = sb.tile([P, 1], F32, name="warm_out")
+        a_raw = tiles(sb, "a_raw", H, [P, ROW_TILES, S], BF16)
+        a_grouped = tiles(sb, "a_grouped", STAGED, [P, Q * PACK], BF16)
+        a_codes = tiles(sb, "a_codes", 2, [P, PASSES, 2 * Q], U32)
+        a_scales = tiles(sb, "a_scales", 2, [P, PASSES, 2 * Q], U8)
+        v_raw = tiles(sb, "v_raw", PASSES, [P, PACK, C], BF16)
+        v_grouped = tiles(sb, "v_grouped", 2, [P, C * PACK], BF16)
+        v_codes = tiles(sb, "v_codes", PASSES, [P, C], U32)
+        v_scales = tiles(sb, "v_scales", PASSES, [P, C], U8)
+        g_raw = tiles(sb, "g_raw", H // 2, [P, PACK, 2 * Q], BF16)
+        sig = tiles(sb, "sig", 2, [P, PACK, 2 * Q], F32)
+        y = sb.tile([P, PACK, H * Q], F32, name="y", align_bytes=256)
+        y_grouped = tiles(sb, "y_grouped", 2, [P, Q * PACK], BF16)
+        y_codes = sb.tile([P, H * Q], U32, name="y_codes", align_bytes=256)
+        y_scales = sb.tile([P, H * Q], U8, name="y_scales", align_bytes=256)
+        turned = tiles(ps, "turned", 4, [P, ROW_TILES, 2, P], F32)
+        acc = tiles(ps, "acc", 4, [P, BANK], F32)
+
+        gate_rows = gate.rearrange("(p t) h q -> p t (h q)", t=PACK)
+        y_rows = out_0.rearrange("(p t) h q -> p t (h q)", t=PACK)
+        word_rows = out_1[0].rearrange("p m t -> p (m t)").bitcast(I32)
+        scale_rows = out_2[0].bitcast(I32)
+
+        def head_cols(h, count=1):
+            return slice(h * Q, (h + count) * Q)
+
+        def load_attn(h, half):
+            ks = slice(half * S // 2, (half + 1) * S // 2)
+            nc.sync.dma_start(out=a_raw[h][:, :, ks], in_=attn[h].rearrange("(r p) k -> p r k", p=P)[:, :, ks])
+
+        def load_values(g):
+            rows = values[g * K_PASS : (g + 1) * K_PASS, :]
+            nc.sync.dma_start(out=v_raw[g][:], in_=rows.rearrange("(p j) c -> p j c", j=PACK))
+
+        def load_gate(pair):
+            nc.sync.dma_start(out=g_raw[pair][:], in_=gate_rows[:, :, head_cols(2 * pair, 2)])
+
+        def group_values(g, on_scalar):
+            cut = P - SCALAR_SHARE[g]
+            ms = slice(cut, P) if on_scalar else slice(0, cut)
+            dst = v_grouped[g % 2][:].rearrange("p (t m j) -> p m t j", t=PACK, j=PACK)[:, ms]
+            src = v_raw[g][:].rearrange("p j (m t) -> p m t j", t=PACK)[:, ms]
+            if not on_scalar:
+                nc.vector.tensor_copy(out=dst, in_=src)
+            elif cut < P:
+                nc.scalar.copy(out=dst, in_=src)
+
+        def quantize_values(g):
+            nc.vector.quantize_mx(out=v_codes[g][:].bitcast(FP8X4), scales=v_scales[g][:], in_=v_grouped[g % 2][:])
+
+        def turn(h, g, bank):
+            for r in range(ROW_TILES):
+                words = a_raw[h][:, r, :].bitcast(F32)
+                for u in range(2):
+                    first = g * K_PASS // 2 + u
+                    nc.tensor.transpose(turned[bank][:, r, u, :], words[:, first : (g + 1) * K_PASS // 2 : 2], ident[:])
+
+        def stage(h, g, bank):
+            dst = a_grouped[(h * PASSES + g) % STAGED][:].bitcast(F32).rearrange("p (r m u) -> p r m u", r=ROW_TILES, u=2)
+            nc.scalar.copy(out=dst, in_=turned[bank][:].rearrange("p r u m -> p r m u"))
+
+        def quantize_attn(h, g):
+            cols = head_cols(h % 2)
+            nc.vector.quantize_mx(
+                out=a_codes[h // 2 % 2][:, g, cols].bitcast(FP8X4),
+                scales=a_scales[h // 2 % 2][:, g, cols],
+                in_=a_grouped[(h * PASSES + g) % STAGED][:],
+            )
+
+        def mx_pass(out, t, g, pair, cols):
+            channels = slice(t * P, (t + 1) * P)
+            nc.tensor.matmul_mx(
+                out=out,
+                lhsT=v_codes[g][:, channels].bitcast(FP8X4),
+                lhsT_scale=v_scales[g][:, channels],
+                rhs=a_codes[pair % 2][:, g, cols].bitcast(FP8X4),
+                rhs_scale=a_scales[pair % 2][:, g, cols],
+                start=(g == 0),
+                stop=(g == PASSES - 1),
+            )
+
+        def multiply_first_pair(g):
+            for t in range(PACK):
+                mx_pass(acc[t][:], t, g, 0, head_cols(0, 2))
+
+        def multiply_head(h):
+            for t in range(PACK):
+                for g in range(PASSES):
+                    mx_pass(acc[2 * (h % 2) + t // 2][:, head_cols(t % 2)], t, g, h // 2, head_cols(h % 2))
+
+        def gate_sigmoid(h, t):
+            cols = head_cols(h % 2)
+            nc.scalar.activation(
+                out=sig[h // 2 % 2][:, t, cols],
+                in_=g_raw[h // 2][:, t, cols],
+                func=SIGMOID,
+                bias=bias[:, t * H + h : t * H + h + 1],
+            )
+
+        def gate_first_pair(t):
+            nc.vector.tensor_tensor(out=y[:, t, head_cols(0, 2)], in0=acc[t][:], in1=sig[0][:, t, :], op=MULT)
+
+        def gate_head(h, b):
+            ts = slice(2 * b, 2 * b + 2)
+            nc.vector.tensor_tensor(
+                out=y[:, ts, head_cols(h)],
+                in0=acc[2 * (h % 2) + b][:].rearrange("p (t q) -> p t q", t=2),
+                in1=sig[h // 2 % 2][:, ts, head_cols(h % 2)],
+                op=MULT,
+            )
+
+        def group_y(h):
+            nc.vector.tensor_copy(
+                out=y_grouped[h % 2][:].rearrange("p (c i t) -> p c t i", i=PACK, t=PACK),
+                in_=y[:, :, head_cols(h)].rearrange("p t (c i) -> p c t i", i=PACK),
+            )
+
+        def quantize_y(h):
+            nc.vector.quantize_mx(
+                out=y_codes[:, head_cols(h)].bitcast(FP8X4), scales=y_scales[:, head_cols(h)], in_=y_grouped[h % 2][:]
+            )
+
+        def store_y(h, count):
+            nc.sync.dma_start(out=y_rows[:, :, head_cols(h, count)], in_=y[:, :, head_cols(h, count)])
+
+        def store_words(h, count):
+            nc.sync.dma_start(out=word_rows[:, head_cols(h, count)], in_=y_codes[:, head_cols(h, count)].bitcast(I32))
+
+        def store_scales(h, count, engine):
+            words = slice(h * Q // 4, (h + count) * Q // 4)
+            for quad in range(4):
+                engine.dma_start(
+                    out=scale_rows[4 * quad : 4 * quad + 4, words],
+                    in_=y_scales[32 * quad : 32 * quad + 4, head_cols(h, count)].bitcast(I32),
+                )
+
+        load_attn(0, 0)
+        load_attn(1, 0)
+        load_values(0)
+        load_values(1)
+        load_attn(0, 1)
+        load_attn(1, 1)
+        load_values(2)
+        load_values(3)
+        for h in range(2, H):
+            load_attn(h, 0)
+            load_attn(h, 1)
+            if h == 2:
+                load_gate(0)
+            if h % 2 == 1:
+                load_gate(h // 2)
+
+        make_identity(nc, ident[:])
+        nc.vector.memset(warm_in[:], 0.0)
+        nc.scalar.dma_start(out=bias[:], in_=gate_bias.rearrange("(p t) h -> p (t h)", t=PACK))
+        nc.scalar.activation(out=warm_out[:], in_=warm_in[:], func=SIGMOID)
+
+        for i, (h, g) in enumerate(((0, 0), (0, 1), (1, 0), (1, 1))):
+            turn(h, g, i)
+            stage(h, g, i)
+        quantize_attn(0, 0)
+        quantize_attn(0, 1)
+        group_values(0, True)
+        group_values(0, False)
+        quantize_attn(1, 0)
+        quantize_values(0)
+        quantize_attn(1, 1)
+        multiply_first_pair(0)
+        group_values(1, True)
+        group_values(1, False)
+        for i, (h, g) in enumerate(((0, 2), (0, 3), (1, 2), (1, 3))):
+            turn(h, g, i)
+            stage(h, g, i)
+        quantize_values(1)
+        multiply_first_pair(1)
+        quantize_attn(0, 2)
+        group_values(2, True)
+        group_values(2, False)
+        quantize_attn(1, 2)
+        quantize_values(2)
+        multiply_first_pair(2)
+        group_values(3, True)
+        group_values(3, False)
+        quantize_attn(0, 3)
+        quantize_attn(1, 3)
+        quantize_values(3)
+        for g in range(PASSES):
+            turn(2, g, g)
+            stage(2, g, g)
+        multiply_first_pair(3)
+        for g in range(PASSES):
+            quantize_attn(2, g)
+        for t in range(PACK):
+            gate_sigmoid(0, t)
+            gate_sigmoid(1, t)
+            gate_first_pair(t)
+        group_y(0)
+
+        for h in range(2, H):
+            if h + 1 < H:
+                for g in range(PASSES):
+                    turn(h + 1, g, g)
+                    stage(h + 1, g, g)
+            for t in range(PACK):
+                gate_sigmoid(h, t)
+            multiply_head(h)
+            if h == 2:
+                quantize_y(0)
+            group_y(h - 1)
+            if h + 1 < H:
+                quantize_attn(h + 1, 0)
+                quantize_attn(h + 1, 1)
+            quantize_y(h - 1)
+            if h + 1 < H:
+                quantize_attn(h + 1, 2)
+                quantize_attn(h + 1, 3)
+            gate_head(h, 0)
+            gate_head(h, 1)
+            if h % 2 == 0 and h < 6:
+                store_y(h - 2, 2)
+                store_words(h - 2, 2)
+            if h >= 5:
+                store_y(h - 1, 1)
+                store_words(h - 1, 1)
+            if h == 6:
+                store_scales(0, 6, nc.sync)
+        store_y(H - 1, 1)
+        group_y(H - 1)
+        quantize_y(H - 1)
+        store_words(H - 1, 1)
+        store_scales(H - 2, 2, nc.scalar)

@@ -22,7 +22,11 @@ PASSES = S // K_PASS
 ROW_TILES = Q // P
 BANK = 512
 STAGED = 8
-SCALAR_SHARE = (32, 32, 0, 32)
+RAW = 8
+VALUE_SHARE = (32, 32, 32, 48)
+Y_SHARE = (0, 0, 24, 24, 24, 0, 64, 24)
+SPLIT_PARTS = ((0, 0, 4, "V"),)
+FIRST_SPLIT = 4
 
 
 def tile_gated_cached_value_mix_g2_kernel(tc, attn, values, gate, gate_bias, out_0, out_1, out_2):
@@ -41,15 +45,16 @@ def tile_gated_cached_value_mix_g2_kernel(tc, attn, values, gate, gate_bias, out
         bias = sb.tile([P, PACK * H], BF16, name="bias", align_bytes=256)
         warm_in = sb.tile([P, 1], F32, name="warm_in")
         warm_out = sb.tile([P, 1], F32, name="warm_out")
-        a_raw = tiles(sb, "a_raw", H, [P, ROW_TILES, S], BF16)
-        a_grouped = tiles(sb, "a_grouped", STAGED, [P, Q * PACK], BF16)
-        a_codes = tiles(sb, "a_codes", 2, [P, PASSES, 2 * Q], U32)
-        a_scales = tiles(sb, "a_scales", 2, [P, PASSES, 2 * Q], U8)
+        a_raw = tiles(sb, "a_raw", RAW, [P, ROW_TILES, S], BF16)
+        a_split = tiles(sb, "a_split", 4, [P, PASSES, 2, P], F32)
+        a_grouped = sb.tile([P, STAGED, Q * PACK], BF16, name="a_grouped", align_bytes=256)
+        a_codes = tiles(sb, "a_codes", 2, [P, STAGED, Q], U32)
+        a_scales = tiles(sb, "a_scales", 2, [P, STAGED, Q], U8)
         v_raw = tiles(sb, "v_raw", PASSES, [P, PACK, C], BF16)
         v_grouped = tiles(sb, "v_grouped", 2, [P, C * PACK], BF16)
         v_codes = tiles(sb, "v_codes", PASSES, [P, C], U32)
         v_scales = tiles(sb, "v_scales", PASSES, [P, C], U8)
-        g_raw = tiles(sb, "g_raw", H // 2, [P, PACK, 2 * Q], BF16)
+        g_raw = sb.tile([P, PACK, H * Q], BF16, name="g_raw", align_bytes=256)
         sig = tiles(sb, "sig", 2, [P, PACK, 2 * Q], F32)
         y = sb.tile([P, PACK, H * Q], F32, name="y", align_bytes=256)
         y_grouped = tiles(sb, "y_grouped", 2, [P, Q * PACK], BF16)
@@ -66,75 +71,113 @@ def tile_gated_cached_value_mix_g2_kernel(tc, attn, values, gate, gate_bias, out
         def head_cols(h, count=1):
             return slice(h * Q, (h + count) * Q)
 
-        def load_attn(h, half):
-            ks = slice(half * S // 2, (half + 1) * S // 2)
-            nc.sync.dma_start(out=a_raw[h][:, :, ks], in_=attn[h].rearrange("(r p) k -> p r k", p=P)[:, :, ks])
+        def load_attn(h, half=None):
+            ks = slice(0, S) if half is None else slice(half * S // 2, (half + 1) * S // 2)
+            nc.sync.dma_start(out=a_raw[h % RAW][:, :, ks], in_=attn[h].rearrange("(p r) k -> p r k", r=ROW_TILES)[:, :, ks])
+
+        def load_bias():
+            nc.sync.dma_start(out=bias[:], in_=gate_bias.rearrange("(p t) h -> p (t h)", t=PACK))
+
+        def copy(on, out, in_):
+            if on == "V":
+                nc.vector.tensor_copy(out=out, in_=in_)
+            else:
+                nc.scalar.copy(out=out, in_=in_)
+
+        def slot(h, g):
+            return 2 * g + h if h < 2 else PASSES * (h % 2) + g
+
+        def split_words(h, r, g0, g1, on):
+            gs = slice(g0, g1)
+            if on == "V":
+                nc.vector.tensor_copy(
+                    out=a_split[2 * (h % 2) + r][:, gs].rearrange("p g u w -> p g w u"),
+                    in_=a_raw[h % RAW][:, r, :].bitcast(F32).rearrange("p (g w u) -> p g w u", g=PASSES, u=2)[:, gs],
+                )
+            else:
+                nc.scalar.copy(
+                    out=a_split[2 * (h % 2) + r][:, gs].bitcast(BF16).rearrange("p g u (w e) -> p g w u e", e=2),
+                    in_=a_raw[h % RAW][:, r, :].rearrange("p (g w u e) -> p g w u e", g=PASSES, u=2, e=2)[:, gs],
+                )
 
         def load_values(g):
             rows = values[g * K_PASS : (g + 1) * K_PASS, :]
             nc.sync.dma_start(out=v_raw[g][:], in_=rows.rearrange("(p j) c -> p j c", j=PACK))
 
-        def load_gate(pair):
-            nc.sync.dma_start(out=g_raw[pair][:], in_=gate_rows[:, :, head_cols(2 * pair, 2)])
+        def load_gate(h, count):
+            nc.sync.dma_start(out=g_raw[:, :, head_cols(h, count)], in_=gate_rows[:, :, head_cols(h, count)])
 
-        def group_values(g, on_scalar):
-            cut = P - SCALAR_SHARE[g]
-            ms = slice(cut, P) if on_scalar else slice(0, cut)
+        def group_values(g, m0, m1, on):
+            ms = slice(m0, m1)
             dst = v_grouped[g % 2][:].rearrange("p (t m j) -> p m t j", t=PACK, j=PACK)[:, ms]
-            src = v_raw[g][:].rearrange("p j (m t) -> p m t j", t=PACK)[:, ms]
-            if not on_scalar:
-                nc.vector.tensor_copy(out=dst, in_=src)
-            elif cut < P:
-                nc.scalar.copy(out=dst, in_=src)
+            copy(on, dst, v_raw[g][:].rearrange("p j (m t) -> p m t j", t=PACK)[:, ms])
 
         def quantize_values(g):
             nc.vector.quantize_mx(out=v_codes[g][:].bitcast(FP8X4), scales=v_scales[g][:], in_=v_grouped[g % 2][:])
 
         def turn(h, g, bank):
             for r in range(ROW_TILES):
-                words = a_raw[h][:, r, :].bitcast(F32)
+                words = a_raw[h % RAW][:, r, :].bitcast(F32)
                 for u in range(2):
-                    first = g * K_PASS // 2 + u
-                    nc.tensor.transpose(turned[bank][:, r, u, :], words[:, first : (g + 1) * K_PASS // 2 : 2], ident[:])
+                    if h >= FIRST_SPLIT and any(r == a and b <= g < c for a, b, c, on in SPLIT_PARTS):
+                        source = a_split[2 * (h % 2) + r][:, g, u, :]
+                    else:
+                        source = words[:, g * K_PASS // 2 + u : (g + 1) * K_PASS // 2 : 2]
+                    nc.tensor.transpose(turned[bank][:, r, u, :], source, ident[:])
 
-        def stage(h, g, bank):
-            dst = a_grouped[(h * PASSES + g) % STAGED][:].bitcast(F32).rearrange("p (r m u) -> p r m u", r=ROW_TILES, u=2)
-            nc.scalar.copy(out=dst, in_=turned[bank][:].rearrange("p r u m -> p r m u"))
+        def stage(h, g, bank, on):
+            dst = a_grouped[:, slot(h, g), :].bitcast(F32).rearrange("p (m r u) -> p m r u", r=ROW_TILES, u=2)
+            copy(on, dst, turned[bank][:].rearrange("p r u m -> p m r u"))
 
-        def quantize_attn(h, g):
-            cols = head_cols(h % 2)
+        def quantize_attn(h, g, count):
+            slots = slice(slot(h, g), slot(h, g) + count)
             nc.vector.quantize_mx(
-                out=a_codes[h // 2 % 2][:, g, cols].bitcast(FP8X4),
-                scales=a_scales[h // 2 % 2][:, g, cols],
-                in_=a_grouped[(h * PASSES + g) % STAGED][:],
+                out=a_codes[h // 2 % 2][:, slots, :].rearrange("p s q -> p (s q)").bitcast(FP8X4),
+                scales=a_scales[h // 2 % 2][:, slots, :].rearrange("p s q -> p (s q)"),
+                in_=a_grouped[:, slots, :].rearrange("p s q -> p (s q)"),
             )
 
-        def mx_pass(out, t, g, pair, cols):
+        def mx_pass(out, t, g, h, heads):
             channels = slice(t * P, (t + 1) * P)
+            slots = slice(slot(h, g), slot(h, g) + heads)
             nc.tensor.matmul_mx(
                 out=out,
                 lhsT=v_codes[g][:, channels].bitcast(FP8X4),
                 lhsT_scale=v_scales[g][:, channels],
-                rhs=a_codes[pair % 2][:, g, cols].bitcast(FP8X4),
-                rhs_scale=a_scales[pair % 2][:, g, cols],
+                rhs=a_codes[h // 2 % 2][:, slots, :].rearrange("p s q -> p (s q)").bitcast(FP8X4),
+                rhs_scale=a_scales[h // 2 % 2][:, slots, :].rearrange("p s q -> p (s q)"),
                 start=(g == 0),
                 stop=(g == PASSES - 1),
             )
 
         def multiply_first_pair(g):
             for t in range(PACK):
-                mx_pass(acc[t][:], t, g, 0, head_cols(0, 2))
+                mx_pass(acc[t][:], t, g, 0, 2)
 
-        def multiply_head(h):
-            for t in range(PACK):
-                for g in range(PASSES):
-                    mx_pass(acc[2 * (h % 2) + t // 2][:, head_cols(t % 2)], t, g, h // 2, head_cols(h % 2))
+        def multiply_slot(h, t):
+            for g in range(PASSES):
+                mx_pass(acc[2 * (h % 2) + t // 2][:, head_cols(t % 2)], t, g, h, 1)
+
+        def last_bank(t):
+            if t < 2:
+                return acc[2 + t][:, 0:Q]
+            return turned[t][:].rearrange("p r u m -> p (r u m)")[:, 0:Q]
+
+        def multiply_last(t):
+            for g in range(PASSES):
+                mx_pass(last_bank(t), t, g, H - 1, 1)
+
+        def gate_last(t):
+            nc.vector.tensor_tensor(out=y[:, t, head_cols(H - 1)], in0=last_bank(t), in1=sig[1][:, t, head_cols(1)], op=MULT)
+
+        def store_y_slots(h, t0, t1):
+            nc.sync.dma_start(out=y_rows[:, t0:t1, head_cols(h)], in_=y[:, t0:t1, head_cols(h)])
 
         def gate_sigmoid(h, t):
             cols = head_cols(h % 2)
             nc.scalar.activation(
                 out=sig[h // 2 % 2][:, t, cols],
-                in_=g_raw[h // 2][:, t, cols],
+                in_=g_raw[:, t, head_cols(h)],
                 func=SIGMOID,
                 bias=bias[:, t * H + h : t * H + h + 1],
             )
@@ -151,11 +194,10 @@ def tile_gated_cached_value_mix_g2_kernel(tc, attn, values, gate, gate_bias, out
                 op=MULT,
             )
 
-        def group_y(h):
-            nc.vector.tensor_copy(
-                out=y_grouped[h % 2][:].rearrange("p (c i t) -> p c t i", i=PACK, t=PACK),
-                in_=y[:, :, head_cols(h)].rearrange("p t (c i) -> p c t i", i=PACK),
-            )
+        def group_y(h, c0, c1, on):
+            cs = slice(c0, c1)
+            dst = y_grouped[h % 2][:].rearrange("p (c i t) -> p c t i", i=PACK, t=PACK)[:, cs]
+            copy(on, dst, y[:, :, head_cols(h)].rearrange("p t (c i) -> p c t i", i=PACK)[:, cs])
 
         def quantize_y(h):
             nc.vector.quantize_mx(
@@ -176,98 +218,133 @@ def tile_gated_cached_value_mix_g2_kernel(tc, attn, values, gate, gate_bias, out
                     in_=y_scales[32 * quad : 32 * quad + 4, head_cols(h, count)].bitcast(I32),
                 )
 
-        load_attn(0, 0)
-        load_attn(1, 0)
-        load_values(0)
-        load_values(1)
-        load_attn(0, 1)
-        load_attn(1, 1)
-        load_values(2)
-        load_values(3)
-        for h in range(2, H):
+
+        for h in range(2):
             load_attn(h, 0)
+        load_values(0)
+        for h in range(2):
             load_attn(h, 1)
-            if h == 2:
-                load_gate(0)
-            if h % 2 == 1:
-                load_gate(h // 2)
+        for g in range(1, PASSES):
+            load_values(g)
+        load_attn(2, 0)
+        load_attn(2, 1)
+        load_bias()
+        load_gate(0, 2)
+        load_attn(3)
+        load_gate(2, 2)
+        load_attn(4)
+        load_attn(5)
+        load_gate(4, 4)
+        load_attn(6)
+        load_attn(7)
 
         make_identity(nc, ident[:])
         nc.vector.memset(warm_in[:], 0.0)
-        nc.scalar.dma_start(out=bias[:], in_=gate_bias.rearrange("(p t) h -> p (t h)", t=PACK))
         nc.scalar.activation(out=warm_out[:], in_=warm_in[:], func=SIGMOID)
 
-        for i, (h, g) in enumerate(((0, 0), (0, 1), (1, 0), (1, 1))):
-            turn(h, g, i)
-            stage(h, g, i)
-        quantize_attn(0, 0)
-        quantize_attn(0, 1)
-        group_values(0, True)
-        group_values(0, False)
-        quantize_attn(1, 0)
+        def share_values(g):
+            group_values(g, P - VALUE_SHARE[g], P, "S")
+            group_values(g, 0, P - VALUE_SHARE[g], "V")
+
+        def share_y(h):
+            if Y_SHARE[h] < Q // PACK:
+                group_y(h, 0, Q // PACK - Y_SHARE[h], "V")
+            if Y_SHARE[h] > 0:
+                group_y(h, Q // PACK - Y_SHARE[h], Q // PACK, "S")
+
+        def split_head(h):
+            for r, g0, g1, on in SPLIT_PARTS:
+                split_words(h, r, g0, g1, on)
+
+        turn(0, 0, 0)
+        stage(0, 0, 0, "S")
+        turn(0, 1, 1)
+        stage(0, 1, 1, "S")
+        turn(1, 0, 2)
+        stage(1, 0, 2, "S")
+        turn(1, 1, 3)
+        share_values(0)
+        stage(1, 1, 3, "S")
+        quantize_attn(0, 0, 2)
         quantize_values(0)
-        quantize_attn(1, 1)
-        multiply_first_pair(0)
-        group_values(1, True)
-        group_values(1, False)
-        for i, (h, g) in enumerate(((0, 2), (0, 3), (1, 2), (1, 3))):
-            turn(h, g, i)
-            stage(h, g, i)
+        quantize_attn(0, 1, 2)
+        turn(0, 2, 0)
+        stage(0, 2, 0, "S")
+        turn(0, 3, 1)
+        stage(0, 3, 1, "S")
+        turn(1, 2, 2)
+        turn(1, 3, 3)
+        share_values(1)
+        stage(1, 2, 2, "S")
         quantize_values(1)
+        multiply_first_pair(0)
         multiply_first_pair(1)
-        quantize_attn(0, 2)
-        group_values(2, True)
-        group_values(2, False)
-        quantize_attn(1, 2)
+        share_values(2)
+        stage(1, 3, 3, "S")
+        quantize_attn(0, 2, 2)
         quantize_values(2)
-        multiply_first_pair(2)
-        group_values(3, True)
-        group_values(3, False)
-        quantize_attn(0, 3)
-        quantize_attn(1, 3)
+        share_values(3)
+        quantize_attn(0, 3, 2)
         quantize_values(3)
         for g in range(PASSES):
             turn(2, g, g)
-            stage(2, g, g)
+            stage(2, g, g, "S")
+        quantize_attn(2, 0, 2)
+        quantize_attn(2, 2, 2)
+        multiply_first_pair(2)
         multiply_first_pair(3)
-        for g in range(PASSES):
-            quantize_attn(2, g)
         for t in range(PACK):
             gate_sigmoid(0, t)
             gate_sigmoid(1, t)
             gate_first_pair(t)
-        group_y(0)
+        share_y(0)
 
-        for h in range(2, H):
-            if h + 1 < H:
-                for g in range(PASSES):
-                    turn(h + 1, g, g)
-                    stage(h + 1, g, g)
-            for t in range(PACK):
-                gate_sigmoid(h, t)
-            multiply_head(h)
+        for h in range(2, H - 1):
+            for g in range(PASSES):
+                turn(h + 1, g, g)
+                stage(h + 1, g, g, "S")
             if h == 2:
+                for t in range(PACK):
+                    gate_sigmoid(2, t)
+                share_y(1)
                 quantize_y(0)
-            group_y(h - 1)
-            if h + 1 < H:
-                quantize_attn(h + 1, 0)
-                quantize_attn(h + 1, 1)
-            quantize_y(h - 1)
-            if h + 1 < H:
-                quantize_attn(h + 1, 2)
-                quantize_attn(h + 1, 3)
+                split_head(4)
+            else:
+                gate_head(h - 1, 1)
+                if h + 2 < H:
+                    split_head(h + 2)
+                share_y(h - 1)
+            quantize_attn(h + 1, 0, 2)
+            if h + 2 == H:
+                quantize_y(h - 1)
+            quantize_attn(h + 1, 2, 2)
+            for t in range(PACK):
+                gate_sigmoid(h + 1, t)
+            for t in range(PACK):
+                multiply_slot(h, t)
             gate_head(h, 0)
-            gate_head(h, 1)
-            if h % 2 == 0 and h < 6:
+            if h + 2 == H:
+                gate_head(h, 1)
+            else:
+                quantize_y(h - 1)
+            if h in (2, 4):
                 store_y(h - 2, 2)
-                store_words(h - 2, 2)
-            if h >= 5:
+            if h > 4:
                 store_y(h - 1, 1)
-                store_words(h - 1, 1)
-            if h == 6:
-                store_scales(0, 6, nc.sync)
-        store_y(H - 1, 1)
-        group_y(H - 1)
+            if h % 2 == 0:
+                store_words(h - 2, 2)
+        store_scales(0, H - 2, nc.sync)
+        store_y_slots(H - 2, 0, 2)
+        store_y_slots(H - 2, 2, 4)
+        share_y(H - 2)
+        for t in range(PACK):
+            multiply_last(t)
+            gate_last(t)
+            if t % 2 == 1:
+                store_y_slots(H - 1, t - 1, t + 1)
+        quantize_y(H - 2)
+        store_words(H - 2, 1)
+        share_y(H - 1)
         quantize_y(H - 1)
         store_words(H - 1, 1)
-        store_scales(H - 2, 2, nc.scalar)
+        store_scales(H - 2, 2, nc.sync)

@@ -23,9 +23,9 @@ ROW_TILES = Q // P
 BANK = 512
 STAGED = 8
 RAW = 8
-VALUE_SHARE = (32, 32, 32, 48)
-Y_SHARE = (0, 0, 24, 24, 24, 0, 64, 24)
-SPLIT_PARTS = ((0, 0, 4, "V"),)
+VALUE_SHARE = (32, 48, 48, 40)
+Y_SHARE = (0, 0, 0, 0, 0, 0, 64, 24)
+SPLIT_PARTS = ((0, 0, 4, "V"), (1, 2, 4, "S"))
 FIRST_SPLIT = 4
 
 
@@ -89,16 +89,11 @@ def tile_gated_cached_value_mix_g2_kernel(tc, attn, values, gate, gate_bias, out
 
         def split_words(h, r, g0, g1, on):
             gs = slice(g0, g1)
-            if on == "V":
-                nc.vector.tensor_copy(
-                    out=a_split[2 * (h % 2) + r][:, gs].rearrange("p g u w -> p g w u"),
-                    in_=a_raw[h % RAW][:, r, :].bitcast(F32).rearrange("p (g w u) -> p g w u", g=PASSES, u=2)[:, gs],
-                )
-            else:
-                nc.scalar.copy(
-                    out=a_split[2 * (h % 2) + r][:, gs].bitcast(BF16).rearrange("p g u (w e) -> p g w u e", e=2),
-                    in_=a_raw[h % RAW][:, r, :].rearrange("p (g w u e) -> p g w u e", g=PASSES, u=2, e=2)[:, gs],
-                )
+            copy(
+                on,
+                a_split[2 * (h % 2) + r][:, gs].rearrange("p g u w -> p g w u"),
+                a_raw[h % RAW][:, r, :].bitcast(F32).rearrange("p (g w u) -> p g w u", g=PASSES, u=2)[:, gs],
+            )
 
         def load_values(g):
             rows = values[g * K_PASS : (g + 1) * K_PASS, :]
@@ -106,6 +101,9 @@ def tile_gated_cached_value_mix_g2_kernel(tc, attn, values, gate, gate_bias, out
 
         def load_gate(h, count):
             nc.sync.dma_start(out=g_raw[:, :, head_cols(h, count)], in_=gate_rows[:, :, head_cols(h, count)])
+
+        def load_gate_slots(t0, t1):
+            nc.sync.dma_start(out=g_raw[:, t0:t1, head_cols(0, 2)], in_=gate_rows[:, t0:t1, head_cols(0, 2)])
 
         def group_values(g, m0, m1, on):
             ms = slice(m0, m1)
@@ -219,16 +217,17 @@ def tile_gated_cached_value_mix_g2_kernel(tc, attn, values, gate, gate_bias, out
                 )
 
 
-        for h in range(2):
-            load_attn(h, 0)
+        load_attn(0, 0)
+        load_attn(1, 0)
         load_values(0)
-        for h in range(2):
-            load_attn(h, 1)
-        for g in range(1, PASSES):
-            load_values(g)
-        load_attn(2, 0)
-        load_attn(2, 1)
+        load_attn(0, 1)
+        load_attn(1, 1)
+        load_values(1)
         load_bias()
+        load_attn(2, 0)
+        load_values(2)
+        load_values(3)
+        load_attn(2, 1)
         load_gate(0, 2)
         load_attn(3)
         load_gate(2, 2)
@@ -278,17 +277,22 @@ def tile_gated_cached_value_mix_g2_kernel(tc, attn, values, gate, gate_bias, out
         stage(1, 2, 2, "S")
         quantize_values(1)
         multiply_first_pair(0)
-        multiply_first_pair(1)
-        share_values(2)
         stage(1, 3, 3, "S")
         quantize_attn(0, 2, 2)
+        turn(2, 0, 0)
+        turn(2, 1, 1)
+        multiply_first_pair(1)
+        share_values(2)
+        stage(2, 0, 0, "S")
+        quantize_attn(0, 3, 2)
         quantize_values(2)
         share_values(3)
-        quantize_attn(0, 3, 2)
+        stage(2, 1, 1, "S")
+        turn(2, 2, 2)
+        stage(2, 2, 2, "S")
+        turn(2, 3, 3)
+        stage(2, 3, 3, "S")
         quantize_values(3)
-        for g in range(PASSES):
-            turn(2, g, g)
-            stage(2, g, g, "S")
         quantize_attn(2, 0, 2)
         quantize_attn(2, 2, 2)
         multiply_first_pair(2)
@@ -303,9 +307,9 @@ def tile_gated_cached_value_mix_g2_kernel(tc, attn, values, gate, gate_bias, out
             for g in range(PASSES):
                 turn(h + 1, g, g)
                 stage(h + 1, g, g, "S")
+            for t in range(PACK):
+                gate_sigmoid(h, t)
             if h == 2:
-                for t in range(PACK):
-                    gate_sigmoid(2, t)
                 share_y(1)
                 quantize_y(0)
                 split_head(4)
@@ -313,13 +317,13 @@ def tile_gated_cached_value_mix_g2_kernel(tc, attn, values, gate, gate_bias, out
                 gate_head(h - 1, 1)
                 if h + 2 < H:
                     split_head(h + 2)
-                share_y(h - 1)
+                    share_y(h - 1)
             quantize_attn(h + 1, 0, 2)
             if h + 2 == H:
-                quantize_y(h - 1)
+                share_y(h - 1)
             quantize_attn(h + 1, 2, 2)
-            for t in range(PACK):
-                gate_sigmoid(h + 1, t)
+            if h + 2 == H:
+                quantize_y(h - 1)
             for t in range(PACK):
                 multiply_slot(h, t)
             gate_head(h, 0)
@@ -336,15 +340,17 @@ def tile_gated_cached_value_mix_g2_kernel(tc, attn, values, gate, gate_bias, out
         store_scales(0, H - 2, nc.sync)
         store_y_slots(H - 2, 0, 2)
         store_y_slots(H - 2, 2, 4)
+        for t in range(PACK):
+            gate_sigmoid(H - 1, t)
         share_y(H - 2)
         for t in range(PACK):
             multiply_last(t)
             gate_last(t)
             if t % 2 == 1:
                 store_y_slots(H - 1, t - 1, t + 1)
+        share_y(H - 1)
         quantize_y(H - 2)
         store_words(H - 2, 1)
-        share_y(H - 1)
         quantize_y(H - 1)
         store_words(H - 1, 1)
         store_scales(H - 2, 2, nc.sync)

@@ -18,15 +18,21 @@ MULT = mybir.AluOpType.mult
 P = 128
 PACK = 4
 K_PASS = P * PACK
+PAIRS = K_PASS // 2
 PASSES = S // K_PASS
-ROW_TILES = Q // P
+ROWS = Q // P
 BANK = 512
-STAGED = 8
-RAW = 8
-VALUE_SHARE = (32, 48, 48, 40)
-Y_SHARE = (0, 0, 0, 0, 0, 0, 64, 24)
-SPLIT_PARTS = ((0, 0, 4, "V"), (1, 2, 4, "S"))
-FIRST_SPLIT = 4
+QUADRANTS = 4
+LAST = H - 1
+
+HALVED_HEADS = 3
+FIRST_SORTED_HEAD = 4
+SORTED_FROM = (0, 2)
+SCALAR_VALUE_SLOTS = (0, 1, 1, 1)
+SCALAR_Y_QUERIES = (0, 64, 0, 0, 0, 0, 192, 96)
+EARLY_QUERIES = 64
+LATER_GATE_LOADS = ((2, 2), (4, 4))
+Y_TILES = ((0, 2), (2, 2), (4, 1), (5, 1), (6, 1), (7, 1))
 
 
 def tile_gated_cached_value_mix_g2_kernel(tc, attn, values, gate, gate_bias, out_0, out_1, out_2):
@@ -36,32 +42,31 @@ def tile_gated_cached_value_mix_g2_kernel(tc, attn, values, gate, gate_bias, out
         ps = ctx.enter_context(tc.psum_pool(name="ps", bufs=1))
         ctx.enter_context(tc.manual_schedule())
 
-        def tiles(pool, name, count, shape, dtype):
-            if pool is ps:
-                return [pool.tile(shape, dtype, name="%s%d" % (name, i)) for i in range(count)]
-            return [pool.tile(shape, dtype, name="%s%d" % (name, i), align_bytes=256) for i in range(count)]
+        def sbuf(name, shape, dtype):
+            return sb.tile(shape, dtype, name=name, align_bytes=256)
 
-        ident = sb.tile([P, P], F32, name="ident", align_bytes=256)
-        bias = sb.tile([P, PACK * H], BF16, name="bias", align_bytes=256)
-        warm_in = sb.tile([P, 1], F32, name="warm_in")
-        warm_out = sb.tile([P, 1], F32, name="warm_out")
-        a_raw = tiles(sb, "a_raw", RAW, [P, ROW_TILES, S], BF16)
-        a_split = tiles(sb, "a_split", 4, [P, PASSES, 2, P], F32)
-        a_grouped = sb.tile([P, STAGED, Q * PACK], BF16, name="a_grouped", align_bytes=256)
-        a_codes = tiles(sb, "a_codes", 2, [P, STAGED, Q], U32)
-        a_scales = tiles(sb, "a_scales", 2, [P, STAGED, Q], U8)
-        v_raw = tiles(sb, "v_raw", PASSES, [P, PACK, C], BF16)
-        v_grouped = tiles(sb, "v_grouped", 2, [P, C * PACK], BF16)
-        v_codes = tiles(sb, "v_codes", PASSES, [P, C], U32)
-        v_scales = tiles(sb, "v_scales", PASSES, [P, C], U8)
-        g_raw = sb.tile([P, PACK, H * Q], BF16, name="g_raw", align_bytes=256)
-        sig = tiles(sb, "sig", 2, [P, PACK, 2 * Q], F32)
-        y = sb.tile([P, PACK, H * Q], F32, name="y", align_bytes=256)
-        y_grouped = tiles(sb, "y_grouped", 2, [P, Q * PACK], BF16)
-        y_codes = sb.tile([P, H * Q], U32, name="y_codes", align_bytes=256)
-        y_scales = sb.tile([P, H * Q], U8, name="y_scales", align_bytes=256)
-        turned = tiles(ps, "turned", 4, [P, ROW_TILES, 2, P], F32)
-        acc = tiles(ps, "acc", 4, [P, BANK], F32)
+        def sbufs(name, count, shape, dtype):
+            return [sbuf("%s%d" % (name, i), shape, dtype) for i in range(count)]
+
+        ident = sbuf("ident", [P, P], F32)
+        bias = sbuf("bias", [P, PACK * H], BF16)
+        a_raw = sbufs("a_raw", H, [P, ROWS * S], BF16)
+        a_sorted = [sbufs("a_sorted%d_" % r, 2, [P, PASSES - SORTED_FROM[r], 2, P], F32) for r in range(ROWS)]
+        a_grouped = sbuf("a_grouped", [P, 2 * PASSES, Q * PACK], BF16)
+        a_codes = sbufs("a_codes", 2, [P, 2 * PASSES, Q], U32)
+        a_scales = sbufs("a_scales", 2, [P, 2 * PASSES, Q], U8)
+        v_raw = sbufs("v_raw", PASSES, [P, PACK, C], BF16)
+        v_grouped = sbufs("v_grouped", 2, [P, C * PACK], BF16)
+        v_codes = sbufs("v_codes", PASSES, [P, C], U32)
+        v_scales = sbufs("v_scales", PASSES, [P, C], U8)
+        g_tiles = {h: sbuf("g_raw%d" % h, [P, PACK, n * Q], BF16) for h, n in ((0, 2),) + LATER_GATE_LOADS}
+        sig = sbufs("sig", 2, [P, 2 * PACK * Q], F32)
+        y_tiles = {h: sbuf("y%d" % h, [P, PACK, n * Q], F32) for h, n in Y_TILES}
+        y_grouped = sbufs("y_grouped", 2, [P, Q * PACK], BF16)
+        y_codes = sbuf("y_codes", [P, H * Q], U32)
+        y_scales = sbuf("y_scales", [P, H * Q], U8)
+        turned = [ps.tile([P, ROWS, 2, P], F32, name="turned%d" % i) for i in range(4)]
+        acc = [ps.tile([P, BANK], F32, name="acc%d" % i) for i in range(4)]
 
         gate_rows = gate.rearrange("(p t) h q -> p t (h q)", t=PACK)
         y_rows = out_0.rearrange("(p t) h q -> p t (h q)", t=PACK)
@@ -71,79 +76,95 @@ def tile_gated_cached_value_mix_g2_kernel(tc, attn, values, gate, gate_bias, out
         def head_cols(h, count=1):
             return slice(h * Q, (h + count) * Q)
 
-        def load_attn(h, half=None):
-            ks = slice(0, S) if half is None else slice(half * S // 2, (half + 1) * S // 2)
-            nc.sync.dma_start(out=a_raw[h % RAW][:, :, ks], in_=attn[h].rearrange("(p r) k -> p r k", r=ROW_TILES)[:, :, ks])
+        def head_of(group, h):
+            first = max(start for start in group if start <= h)
+            return group[first][:, :, head_cols(h - first)]
 
-        def load_bias():
-            nc.sync.dma_start(out=bias[:], in_=gate_bias.rearrange("(p t) h -> p (t h)", t=PACK))
+        def sig_of(h):
+            if h < 2:
+                return sig[0][:].rearrange("p (t m) -> p t m", t=PACK)[:, :, head_cols(h)]
+            return sig[h // 2 % 2][:].rearrange("p (x t q) -> p x t q", x=2, t=PACK)[:, h % 2]
 
-        def copy(on, out, in_):
-            if on == "V":
-                nc.vector.tensor_copy(out=out, in_=in_)
-            else:
-                nc.scalar.copy(out=out, in_=in_)
-
-        def slot(h, g):
+        def cell(h, g):
             return 2 * g + h if h < 2 else PASSES * (h % 2) + g
 
-        def split_words(h, r, g0, g1, on):
-            gs = slice(g0, g1)
-            copy(
-                on,
-                a_split[2 * (h % 2) + r][:, gs].rearrange("p g u w -> p g w u"),
-                a_raw[h % RAW][:, r, :].bitcast(F32).rearrange("p (g w u) -> p g w u", g=PASSES, u=2)[:, gs],
-            )
+        def cells(tile, h, g, count):
+            return tile[:, cell(h, g) : cell(h, g) + count, :].rearrange("p s q -> p (s q)")
+
+        def raw_pairs(h, r, g):
+            if h < HALVED_HEADS:
+                return a_raw[h][:].bitcast(F32).rearrange("p (x r g w) -> p x r g w", x=2, r=ROWS, w=PAIRS)[:, g // 2, r, g % 2]
+            return a_raw[h][:].bitcast(F32).rearrange("p (r g w) -> p r g w", r=ROWS, w=PAIRS)[:, r, g]
+
+        def load_attn(h):
+            nc.sync.dma_start(out=a_raw[h][:], in_=attn[h].rearrange("(p r) k -> p (r k)", r=ROWS))
+
+        def load_attn_half(h, x):
+            rows = attn[h].rearrange("(p r) k -> p r k", r=ROWS)[:, :, x * S // 2 : (x + 1) * S // 2]
+            nc.sync.dma_start(out=a_raw[h][:, x * S : (x + 1) * S].rearrange("p (r k) -> p r k", r=ROWS), in_=rows)
 
         def load_values(g):
             rows = values[g * K_PASS : (g + 1) * K_PASS, :]
             nc.sync.dma_start(out=v_raw[g][:], in_=rows.rearrange("(p j) c -> p j c", j=PACK))
 
-        def load_gate(h, count):
-            nc.sync.dma_start(out=g_raw[:, :, head_cols(h, count)], in_=gate_rows[:, :, head_cols(h, count)])
+        def load_first_gates(slots, cols):
+            nc.sync.dma_start(out=g_tiles[0][:, slots, cols], in_=gate_rows[:, slots, cols])
 
-        def load_gate_slots(t0, t1):
-            nc.sync.dma_start(out=g_raw[:, t0:t1, head_cols(0, 2)], in_=gate_rows[:, t0:t1, head_cols(0, 2)])
+        def load_gates(h, count):
+            nc.sync.dma_start(out=g_tiles[h][:], in_=gate_rows[:, :, head_cols(h, count)])
 
-        def group_values(g, m0, m1, on):
-            ms = slice(m0, m1)
-            dst = v_grouped[g % 2][:].rearrange("p (t m j) -> p m t j", t=PACK, j=PACK)[:, ms]
-            copy(on, dst, v_raw[g][:].rearrange("p j (m t) -> p m t j", t=PACK)[:, ms])
+        def group_values(g):
+            dst = v_grouped[g % 2][:].rearrange("p (t m j) -> p m t j", t=PACK, j=PACK)
+            src = v_raw[g][:].rearrange("p j (m t) -> p m t j", t=PACK)
+            cut = PACK - SCALAR_VALUE_SLOTS[g]
+            if cut < PACK:
+                nc.scalar.copy(out=dst[:, :, cut:], in_=src[:, :, cut:])
+            nc.vector.tensor_copy(out=dst[:, :, :cut], in_=src[:, :, :cut])
 
         def quantize_values(g):
             nc.vector.quantize_mx(out=v_codes[g][:].bitcast(FP8X4), scales=v_scales[g][:], in_=v_grouped[g % 2][:])
 
+        def sort_pairs(h, r):
+            dst = a_sorted[r][h % 2][:].rearrange("p n u w -> p n w u")
+            row = a_raw[h][:, r * S + SORTED_FROM[r] * K_PASS : (r + 1) * S]
+            src = row.bitcast(F32).rearrange("p (n w u) -> p n w u", w=P, u=2)
+            if r == 0:
+                nc.vector.tensor_copy(out=dst, in_=src)
+            else:
+                nc.scalar.copy(out=dst, in_=src)
+
         def turn(h, g, bank):
-            for r in range(ROW_TILES):
-                words = a_raw[h % RAW][:, r, :].bitcast(F32)
+            for r in range(ROWS):
                 for u in range(2):
-                    if h >= FIRST_SPLIT and any(r == a and b <= g < c for a, b, c, on in SPLIT_PARTS):
-                        source = a_split[2 * (h % 2) + r][:, g, u, :]
+                    if h >= FIRST_SORTED_HEAD and g >= SORTED_FROM[r]:
+                        source = a_sorted[r][h % 2][:, g - SORTED_FROM[r], u, :]
                     else:
-                        source = words[:, g * K_PASS // 2 + u : (g + 1) * K_PASS // 2 : 2]
+                        source = raw_pairs(h, r, g)[:, u:PAIRS:2]
                     nc.tensor.transpose(turned[bank][:, r, u, :], source, ident[:])
 
-        def stage(h, g, bank, on):
-            dst = a_grouped[:, slot(h, g), :].bitcast(F32).rearrange("p (m r u) -> p m r u", r=ROW_TILES, u=2)
-            copy(on, dst, turned[bank][:].rearrange("p r u m -> p m r u"))
+        def stage(h, g, bank):
+            dst = cells(a_grouped, h, g, 1).bitcast(F32).rearrange("p (m r u) -> p m r u", r=ROWS, u=2)
+            nc.scalar.copy(out=dst, in_=turned[bank][:].rearrange("p r u m -> p m r u"))
 
-        def quantize_attn(h, g, count):
-            slots = slice(slot(h, g), slot(h, g) + count)
+        def turn_and_stage(h, g, bank):
+            turn(h, g, bank)
+            stage(h, g, bank)
+
+        def quantize_attn(h, g):
             nc.vector.quantize_mx(
-                out=a_codes[h // 2 % 2][:, slots, :].rearrange("p s q -> p (s q)").bitcast(FP8X4),
-                scales=a_scales[h // 2 % 2][:, slots, :].rearrange("p s q -> p (s q)"),
-                in_=a_grouped[:, slots, :].rearrange("p s q -> p (s q)"),
+                out=cells(a_codes[h // 2 % 2], h, g, 2).bitcast(FP8X4),
+                scales=cells(a_scales[h // 2 % 2], h, g, 2),
+                in_=cells(a_grouped, h, g, 2),
             )
 
         def mx_pass(out, t, g, h, heads):
             channels = slice(t * P, (t + 1) * P)
-            slots = slice(slot(h, g), slot(h, g) + heads)
             nc.tensor.matmul_mx(
                 out=out,
                 lhsT=v_codes[g][:, channels].bitcast(FP8X4),
                 lhsT_scale=v_scales[g][:, channels],
-                rhs=a_codes[h // 2 % 2][:, slots, :].rearrange("p s q -> p (s q)").bitcast(FP8X4),
-                rhs_scale=a_scales[h // 2 % 2][:, slots, :].rearrange("p s q -> p (s q)"),
+                rhs=cells(a_codes[h // 2 % 2], h, g, heads).bitcast(FP8X4),
+                rhs_scale=cells(a_scales[h // 2 % 2], h, g, heads),
                 start=(g == 0),
                 stop=(g == PASSES - 1),
             )
@@ -152,50 +173,39 @@ def tile_gated_cached_value_mix_g2_kernel(tc, attn, values, gate, gate_bias, out
             for t in range(PACK):
                 mx_pass(acc[t][:], t, g, 0, 2)
 
-        def multiply_slot(h, t):
-            for g in range(PASSES):
-                mx_pass(acc[2 * (h % 2) + t // 2][:, head_cols(t % 2)], t, g, h, 1)
+        def multiply_head(h):
+            for t in range(PACK):
+                for g in range(PASSES):
+                    mx_pass(acc[2 * (h % 2) + t // 2][:, head_cols(t % 2)], t, g, h, 1)
 
         def last_bank(t):
             if t < 2:
-                return acc[2 + t][:, 0:Q]
-            return turned[t][:].rearrange("p r u m -> p (r u m)")[:, 0:Q]
+                return acc[2 + t][:, :Q]
+            return turned[t][:].rearrange("p r u m -> p (r u m)")[:, :Q]
 
-        def multiply_last(t):
-            for g in range(PASSES):
-                mx_pass(last_bank(t), t, g, H - 1, 1)
-
-        def gate_last(t):
-            nc.vector.tensor_tensor(out=y[:, t, head_cols(H - 1)], in0=last_bank(t), in1=sig[1][:, t, head_cols(1)], op=MULT)
-
-        def store_y_slots(h, t0, t1):
-            nc.sync.dma_start(out=y_rows[:, t0:t1, head_cols(h)], in_=y[:, t0:t1, head_cols(h)])
-
-        def gate_sigmoid(h, t):
-            cols = head_cols(h % 2)
+        def gate_sigmoid(h, t, queries=slice(0, Q)):
             nc.scalar.activation(
-                out=sig[h // 2 % 2][:, t, cols],
-                in_=g_raw[:, t, head_cols(h)],
+                out=sig_of(h)[:, t, queries],
+                in_=head_of(g_tiles, h)[:, t, queries],
                 func=SIGMOID,
                 bias=bias[:, t * H + h : t * H + h + 1],
             )
 
-        def gate_first_pair(t):
-            nc.vector.tensor_tensor(out=y[:, t, head_cols(0, 2)], in0=acc[t][:], in1=sig[0][:, t, :], op=MULT)
+        def apply_gate(out, sums, gates):
+            nc.vector.tensor_tensor(out=out, in0=sums, in1=gates, op=MULT)
 
-        def gate_head(h, b):
-            ts = slice(2 * b, 2 * b + 2)
-            nc.vector.tensor_tensor(
-                out=y[:, ts, head_cols(h)],
-                in0=acc[2 * (h % 2) + b][:].rearrange("p (t q) -> p t q", t=2),
-                in1=sig[h // 2 % 2][:, ts, head_cols(h % 2)],
-                op=MULT,
-            )
+        def gate_bank(h, b):
+            slots = slice(2 * b, 2 * b + 2)
+            sums = acc[2 * (h % 2) + b][:].rearrange("p (t q) -> p t q", t=2)
+            apply_gate(head_of(y_tiles, h)[:, slots, :], sums, sig_of(h)[:, slots, :])
 
-        def group_y(h, c0, c1, on):
-            cs = slice(c0, c1)
-            dst = y_grouped[h % 2][:].rearrange("p (c i t) -> p c t i", i=PACK, t=PACK)[:, cs]
-            copy(on, dst, y[:, :, head_cols(h)].rearrange("p t (c i) -> p c t i", i=PACK)[:, cs])
+        def group_y(h):
+            dst = y_grouped[h % 2][:].rearrange("p (c i t) -> p c t i", i=PACK, t=PACK)
+            src = head_of(y_tiles, h).rearrange("p t (c i) -> p c t i", i=PACK)
+            cut = (Q - SCALAR_Y_QUERIES[h]) // PACK
+            nc.vector.tensor_copy(out=dst[:, :cut], in_=src[:, :cut])
+            if cut < Q // PACK:
+                nc.scalar.copy(out=dst[:, cut:], in_=src[:, cut:])
 
         def quantize_y(h):
             nc.vector.quantize_mx(
@@ -203,154 +213,130 @@ def tile_gated_cached_value_mix_g2_kernel(tc, attn, values, gate, gate_bias, out
             )
 
         def store_y(h, count):
-            nc.sync.dma_start(out=y_rows[:, :, head_cols(h, count)], in_=y[:, :, head_cols(h, count)])
+            nc.sync.dma_start(out=y_rows[:, :, head_cols(h, count)], in_=y_tiles[h][:])
+
+        def store_y_slots(h, t0):
+            nc.sync.dma_start(out=y_rows[:, t0 : t0 + 2, head_cols(h)], in_=y_tiles[h][:, t0 : t0 + 2, :])
 
         def store_words(h, count):
             nc.sync.dma_start(out=word_rows[:, head_cols(h, count)], in_=y_codes[:, head_cols(h, count)].bitcast(I32))
 
-        def store_scales(h, count, engine):
-            words = slice(h * Q // 4, (h + count) * Q // 4)
-            for quad in range(4):
-                engine.dma_start(
-                    out=scale_rows[4 * quad : 4 * quad + 4, words],
-                    in_=y_scales[32 * quad : 32 * quad + 4, head_cols(h, count)].bitcast(I32),
+        def store_scales(h, count, queues):
+            for n in range(QUADRANTS):
+                queues[n % len(queues)].dma_start(
+                    out=scale_rows[4 * n : 4 * n + 4, h * Q // 4 : (h + count) * Q // 4],
+                    in_=y_scales[32 * n : 32 * n + 4, head_cols(h, count)].bitcast(I32),
                 )
 
-
-        load_attn(0, 0)
-        load_attn(1, 0)
+        load_attn_half(0, 0)
+        nc.sync.dma_start(out=bias[:], in_=gate_bias.rearrange("(p t) h -> p (t h)", t=PACK))
+        load_first_gates(slice(0, 1), slice(0, EARLY_QUERIES))
+        load_attn_half(1, 0)
         load_values(0)
-        load_attn(0, 1)
-        load_attn(1, 1)
+        load_attn_half(0, 1)
+        load_attn_half(1, 1)
         load_values(1)
-        load_bias()
-        load_attn(2, 0)
         load_values(2)
         load_values(3)
-        load_attn(2, 1)
-        load_gate(0, 2)
+        load_attn_half(2, 0)
+        load_attn_half(2, 1)
+        load_first_gates(slice(0, 1), slice(EARLY_QUERIES, 2 * Q))
+        load_first_gates(slice(1, PACK), slice(0, 2 * Q))
         load_attn(3)
-        load_gate(2, 2)
         load_attn(4)
+        load_gates(*LATER_GATE_LOADS[0])
         load_attn(5)
-        load_gate(4, 4)
+        load_gates(*LATER_GATE_LOADS[1])
         load_attn(6)
         load_attn(7)
 
         make_identity(nc, ident[:])
-        nc.vector.memset(warm_in[:], 0.0)
-        nc.scalar.activation(out=warm_out[:], in_=warm_in[:], func=SIGMOID)
+        gate_sigmoid(0, 0, slice(0, EARLY_QUERIES))
 
-        def share_values(g):
-            group_values(g, P - VALUE_SHARE[g], P, "S")
-            group_values(g, 0, P - VALUE_SHARE[g], "V")
-
-        def share_y(h):
-            if Y_SHARE[h] < Q // PACK:
-                group_y(h, 0, Q // PACK - Y_SHARE[h], "V")
-            if Y_SHARE[h] > 0:
-                group_y(h, Q // PACK - Y_SHARE[h], Q // PACK, "S")
-
-        def split_head(h):
-            for r, g0, g1, on in SPLIT_PARTS:
-                split_words(h, r, g0, g1, on)
-
-        turn(0, 0, 0)
-        stage(0, 0, 0, "S")
-        turn(0, 1, 1)
-        stage(0, 1, 1, "S")
-        turn(1, 0, 2)
-        stage(1, 0, 2, "S")
-        turn(1, 1, 3)
-        share_values(0)
-        stage(1, 1, 3, "S")
-        quantize_attn(0, 0, 2)
+        turn_and_stage(0, 0, 0)
+        turn_and_stage(0, 1, 1)
+        turn_and_stage(1, 0, 2)
+        turn_and_stage(1, 1, 3)
+        group_values(0)
+        quantize_attn(0, 0)
         quantize_values(0)
-        quantize_attn(0, 1, 2)
-        turn(0, 2, 0)
-        stage(0, 2, 0, "S")
-        turn(0, 3, 1)
-        stage(0, 3, 1, "S")
-        turn(1, 2, 2)
-        turn(1, 3, 3)
-        share_values(1)
-        stage(1, 2, 2, "S")
+        quantize_attn(0, 1)
+        turn_and_stage(0, 2, 0)
+        turn_and_stage(0, 3, 1)
+        group_values(1)
+        turn_and_stage(1, 2, 2)
         quantize_values(1)
         multiply_first_pair(0)
-        stage(1, 3, 3, "S")
-        quantize_attn(0, 2, 2)
-        turn(2, 0, 0)
-        turn(2, 1, 1)
+        turn(1, 3, 3)
         multiply_first_pair(1)
-        share_values(2)
-        stage(2, 0, 0, "S")
-        quantize_attn(0, 3, 2)
+        group_values(2)
+        quantize_attn(0, 2)
+        group_values(3)
+        stage(1, 3, 3)
         quantize_values(2)
-        share_values(3)
-        stage(2, 1, 1, "S")
-        turn(2, 2, 2)
-        stage(2, 2, 2, "S")
-        turn(2, 3, 3)
-        stage(2, 3, 3, "S")
         quantize_values(3)
-        quantize_attn(2, 0, 2)
-        quantize_attn(2, 2, 2)
+        quantize_attn(0, 3)
+        for g in range(PASSES):
+            turn_and_stage(2, g, g)
+        quantize_attn(2, 0)
+        quantize_attn(2, 2)
         multiply_first_pair(2)
         multiply_first_pair(3)
         for t in range(PACK):
-            gate_sigmoid(0, t)
+            gate_sigmoid(0, t, slice(EARLY_QUERIES if t == 0 else 0, Q))
             gate_sigmoid(1, t)
-            gate_first_pair(t)
-        share_y(0)
+            apply_gate(y_tiles[0][:, t, :], acc[t][:], sig[0][:, t * BANK : (t + 1) * BANK])
+        sort_pairs(FIRST_SORTED_HEAD, 0)
+        group_y(0)
 
-        for h in range(2, H - 1):
+        for h in range(2, LAST):
+            next_is_last = h + 1 == LAST
             for g in range(PASSES):
-                turn(h + 1, g, g)
-                stage(h + 1, g, g, "S")
+                turn_and_stage(h + 1, g, g)
             for t in range(PACK):
                 gate_sigmoid(h, t)
             if h == 2:
-                share_y(1)
+                sort_pairs(FIRST_SORTED_HEAD, 1)
+                group_y(1)
                 quantize_y(0)
-                split_head(4)
             else:
-                gate_head(h - 1, 1)
-                if h + 2 < H:
-                    split_head(h + 2)
-                    share_y(h - 1)
-            quantize_attn(h + 1, 0, 2)
-            if h + 2 == H:
-                share_y(h - 1)
-            quantize_attn(h + 1, 2, 2)
-            if h + 2 == H:
+                gate_bank(h - 1, 1)
+                if not next_is_last:
+                    sort_pairs(h + 2, 0)
+                    sort_pairs(h + 2, 1)
+                    group_y(h - 1)
+            quantize_attn(h + 1, 0)
+            if next_is_last:
+                group_y(h - 1)
+            quantize_attn(h + 1, 2)
+            if next_is_last:
                 quantize_y(h - 1)
-            for t in range(PACK):
-                multiply_slot(h, t)
-            gate_head(h, 0)
-            if h + 2 == H:
-                gate_head(h, 1)
+            multiply_head(h)
+            gate_bank(h, 0)
+            if next_is_last:
+                gate_bank(h, 1)
             else:
                 quantize_y(h - 1)
-            if h in (2, 4):
-                store_y(h - 2, 2)
-            if h > 4:
-                store_y(h - 1, 1)
+            for first, count in Y_TILES:
+                if first + count == h:
+                    store_y(first, count)
             if h % 2 == 0:
                 store_words(h - 2, 2)
-        store_scales(0, H - 2, nc.sync)
-        store_y_slots(H - 2, 0, 2)
-        store_y_slots(H - 2, 2, 4)
+        store_scales(0, LAST - 1, [nc.sync])
+        store_y_slots(LAST - 1, 0)
+        store_y_slots(LAST - 1, 2)
+
         for t in range(PACK):
-            gate_sigmoid(H - 1, t)
-        share_y(H - 2)
+            gate_sigmoid(LAST, t)
         for t in range(PACK):
-            multiply_last(t)
-            gate_last(t)
+            for g in range(PASSES):
+                mx_pass(last_bank(t), t, g, LAST, 1)
+            apply_gate(y_tiles[LAST][:, t, :], last_bank(t), sig_of(LAST)[:, t, :])
             if t % 2 == 1:
-                store_y_slots(H - 1, t - 1, t + 1)
-        share_y(H - 1)
-        quantize_y(H - 2)
-        store_words(H - 2, 1)
-        quantize_y(H - 1)
-        store_words(H - 1, 1)
-        store_scales(H - 2, 2, nc.sync)
+                store_y_slots(LAST, t - 1)
+        group_y(LAST - 1)
+        group_y(LAST)
+        for h in (LAST - 1, LAST):
+            quantize_y(h)
+            store_words(h, 1)
+        store_scales(LAST - 1, 2, [nc.scalar, nc.sync])

from contextlib import ExitStack

import concourse.mybir as mybir
from concourse.masks import make_identity

S, C, H, Q = 2048, 512, 8, 256
FLOPS = 2 * C * H * Q * S

F32 = mybir.dt.float32
BF16 = mybir.dt.bfloat16
I32 = mybir.dt.int32
U32 = mybir.dt.uint32
U8 = mybir.dt.uint8
FP8X4 = mybir.dt.float8_e4m3fn_x4
SIGMOID = mybir.ActivationFunctionType.Sigmoid
MULT = mybir.AluOpType.mult

P = 128
PACK = 4
K_PASS = P * PACK
PAIRS = K_PASS // 2
PASSES = S // K_PASS
ROWS = Q // P
BANK = 512
QUADRANTS = 4
LAST = H - 1

HALVED_HEADS = 3
FIRST_SORTED_HEAD = 4
SORTED_FROM = (0, 2)
SCALAR_VALUE_SLOTS = (0, 1, 1, 1)
SCALAR_Y_QUERIES = (0, 64, 0, 0, 0, 0, 192, 96)
EARLY_QUERIES = 64
LATER_GATE_LOADS = ((2, 2), (4, 4))
Y_TILES = ((0, 2), (2, 2), (4, 1), (5, 1), (6, 1), (7, 1))


def tile_gated_cached_value_mix_g2_kernel(tc, attn, values, gate, gate_bias, out_0, out_1, out_2):
    nc = tc.nc
    with ExitStack() as ctx:
        sb = ctx.enter_context(tc.tile_pool(name="sb", bufs=1))
        ps = ctx.enter_context(tc.psum_pool(name="ps", bufs=1))
        ctx.enter_context(tc.manual_schedule())

        def sbuf(name, shape, dtype):
            return sb.tile(shape, dtype, name=name, align_bytes=256)

        def sbufs(name, count, shape, dtype):
            return [sbuf("%s%d" % (name, i), shape, dtype) for i in range(count)]

        ident = sbuf("ident", [P, P], F32)
        bias = sbuf("bias", [P, PACK * H], BF16)
        a_raw = sbufs("a_raw", H, [P, ROWS * S], BF16)
        a_sorted = [sbufs("a_sorted%d_" % r, 2, [P, PASSES - SORTED_FROM[r], 2, P], F32) for r in range(ROWS)]
        a_grouped = sbuf("a_grouped", [P, 2 * PASSES, Q * PACK], BF16)
        a_codes = sbufs("a_codes", 2, [P, 2 * PASSES, Q], U32)
        a_scales = sbufs("a_scales", 2, [P, 2 * PASSES, Q], U8)
        v_raw = sbufs("v_raw", PASSES, [P, PACK, C], BF16)
        v_grouped = sbufs("v_grouped", 2, [P, C * PACK], BF16)
        v_codes = sbufs("v_codes", PASSES, [P, C], U32)
        v_scales = sbufs("v_scales", PASSES, [P, C], U8)
        g_tiles = {h: sbuf("g_raw%d" % h, [P, PACK, n * Q], BF16) for h, n in ((0, 2),) + LATER_GATE_LOADS}
        sig = sbufs("sig", 2, [P, 2 * PACK * Q], F32)
        y_tiles = {h: sbuf("y%d" % h, [P, PACK, n * Q], F32) for h, n in Y_TILES}
        y_grouped = sbufs("y_grouped", 2, [P, Q * PACK], BF16)
        y_codes = sbuf("y_codes", [P, H * Q], U32)
        y_scales = sbuf("y_scales", [P, H * Q], U8)
        turned = [ps.tile([P, ROWS, 2, P], F32, name="turned%d" % i) for i in range(4)]
        acc = [ps.tile([P, BANK], F32, name="acc%d" % i) for i in range(4)]

        gate_rows = gate.rearrange("(p t) h q -> p t (h q)", t=PACK)
        y_rows = out_0.rearrange("(p t) h q -> p t (h q)", t=PACK)
        word_rows = out_1[0].rearrange("p m t -> p (m t)").bitcast(I32)
        scale_rows = out_2[0].bitcast(I32)

        def head_cols(h, count=1):
            return slice(h * Q, (h + count) * Q)

        def head_of(group, h):
            first = max(start for start in group if start <= h)
            return group[first][:, :, head_cols(h - first)]

        def sig_of(h):
            if h < 2:
                return sig[0][:].rearrange("p (t m) -> p t m", t=PACK)[:, :, head_cols(h)]
            return sig[h // 2 % 2][:].rearrange("p (x t q) -> p x t q", x=2, t=PACK)[:, h % 2]

        def cell(h, g):
            return 2 * g + h if h < 2 else PASSES * (h % 2) + g

        def cells(tile, h, g, count):
            return tile[:, cell(h, g) : cell(h, g) + count, :].rearrange("p s q -> p (s q)")

        def raw_pairs(h, r, g):
            if h < HALVED_HEADS:
                return a_raw[h][:].bitcast(F32).rearrange("p (x r g w) -> p x r g w", x=2, r=ROWS, w=PAIRS)[:, g // 2, r, g % 2]
            return a_raw[h][:].bitcast(F32).rearrange("p (r g w) -> p r g w", r=ROWS, w=PAIRS)[:, r, g]

        def load_attn(h):
            nc.sync.dma_start(out=a_raw[h][:], in_=attn[h].rearrange("(p r) k -> p (r k)", r=ROWS))

        def load_attn_half(h, x):
            rows = attn[h].rearrange("(p r) k -> p r k", r=ROWS)[:, :, x * S // 2 : (x + 1) * S // 2]
            nc.sync.dma_start(out=a_raw[h][:, x * S : (x + 1) * S].rearrange("p (r k) -> p r k", r=ROWS), in_=rows)

        def load_values(g):
            rows = values[g * K_PASS : (g + 1) * K_PASS, :]
            nc.sync.dma_start(out=v_raw[g][:], in_=rows.rearrange("(p j) c -> p j c", j=PACK))

        def load_first_gates(slots, cols):
            nc.sync.dma_start(out=g_tiles[0][:, slots, cols], in_=gate_rows[:, slots, cols])

        def load_gates(h, count):
            nc.sync.dma_start(out=g_tiles[h][:], in_=gate_rows[:, :, head_cols(h, count)])

        def group_values(g):
            dst = v_grouped[g % 2][:].rearrange("p (t m j) -> p m t j", t=PACK, j=PACK)
            src = v_raw[g][:].rearrange("p j (m t) -> p m t j", t=PACK)
            cut = PACK - SCALAR_VALUE_SLOTS[g]
            if cut < PACK:
                nc.scalar.copy(out=dst[:, :, cut:], in_=src[:, :, cut:])
            nc.vector.tensor_copy(out=dst[:, :, :cut], in_=src[:, :, :cut])

        def quantize_values(g):
            nc.vector.quantize_mx(out=v_codes[g][:].bitcast(FP8X4), scales=v_scales[g][:], in_=v_grouped[g % 2][:])

        def sort_pairs(h, r):
            dst = a_sorted[r][h % 2][:].rearrange("p n u w -> p n w u")
            row = a_raw[h][:, r * S + SORTED_FROM[r] * K_PASS : (r + 1) * S]
            src = row.bitcast(F32).rearrange("p (n w u) -> p n w u", w=P, u=2)
            if r == 0:
                nc.vector.tensor_copy(out=dst, in_=src)
            else:
                nc.scalar.copy(out=dst, in_=src)

        def turn(h, g, bank):
            for r in range(ROWS):
                for u in range(2):
                    if h >= FIRST_SORTED_HEAD and g >= SORTED_FROM[r]:
                        source = a_sorted[r][h % 2][:, g - SORTED_FROM[r], u, :]
                    else:
                        source = raw_pairs(h, r, g)[:, u:PAIRS:2]
                    nc.tensor.transpose(turned[bank][:, r, u, :], source, ident[:])

        def stage(h, g, bank):
            dst = cells(a_grouped, h, g, 1).bitcast(F32).rearrange("p (m r u) -> p m r u", r=ROWS, u=2)
            nc.scalar.copy(out=dst, in_=turned[bank][:].rearrange("p r u m -> p m r u"))

        def turn_and_stage(h, g, bank):
            turn(h, g, bank)
            stage(h, g, bank)

        def quantize_attn(h, g):
            nc.vector.quantize_mx(
                out=cells(a_codes[h // 2 % 2], h, g, 2).bitcast(FP8X4),
                scales=cells(a_scales[h // 2 % 2], h, g, 2),
                in_=cells(a_grouped, h, g, 2),
            )

        def mx_pass(out, t, g, h, heads):
            channels = slice(t * P, (t + 1) * P)
            nc.tensor.matmul_mx(
                out=out,
                lhsT=v_codes[g][:, channels].bitcast(FP8X4),
                lhsT_scale=v_scales[g][:, channels],
                rhs=cells(a_codes[h // 2 % 2], h, g, heads).bitcast(FP8X4),
                rhs_scale=cells(a_scales[h // 2 % 2], h, g, heads),
                start=(g == 0),
                stop=(g == PASSES - 1),
            )

        def multiply_first_pair(g):
            for t in range(PACK):
                mx_pass(acc[t][:], t, g, 0, 2)

        def multiply_head(h):
            for t in range(PACK):
                for g in range(PASSES):
                    mx_pass(acc[2 * (h % 2) + t // 2][:, head_cols(t % 2)], t, g, h, 1)

        def last_bank(t):
            if t < 2:
                return acc[2 + t][:, :Q]
            return turned[t][:].rearrange("p r u m -> p (r u m)")[:, :Q]

        def gate_sigmoid(h, t, queries=slice(0, Q)):
            nc.scalar.activation(
                out=sig_of(h)[:, t, queries],
                in_=head_of(g_tiles, h)[:, t, queries],
                func=SIGMOID,
                bias=bias[:, t * H + h : t * H + h + 1],
            )

        def apply_gate(out, sums, gates):
            nc.vector.tensor_tensor(out=out, in0=sums, in1=gates, op=MULT)

        def gate_bank(h, b):
            slots = slice(2 * b, 2 * b + 2)
            sums = acc[2 * (h % 2) + b][:].rearrange("p (t q) -> p t q", t=2)
            apply_gate(head_of(y_tiles, h)[:, slots, :], sums, sig_of(h)[:, slots, :])

        def group_y(h):
            dst = y_grouped[h % 2][:].rearrange("p (c i t) -> p c t i", i=PACK, t=PACK)
            src = head_of(y_tiles, h).rearrange("p t (c i) -> p c t i", i=PACK)
            cut = (Q - SCALAR_Y_QUERIES[h]) // PACK
            nc.vector.tensor_copy(out=dst[:, :cut], in_=src[:, :cut])
            if cut < Q // PACK:
                nc.scalar.copy(out=dst[:, cut:], in_=src[:, cut:])

        def quantize_y(h):
            nc.vector.quantize_mx(
                out=y_codes[:, head_cols(h)].bitcast(FP8X4), scales=y_scales[:, head_cols(h)], in_=y_grouped[h % 2][:]
            )

        def store_y(h, count):
            nc.sync.dma_start(out=y_rows[:, :, head_cols(h, count)], in_=y_tiles[h][:])

        def store_y_slots(h, t0):
            nc.sync.dma_start(out=y_rows[:, t0 : t0 + 2, head_cols(h)], in_=y_tiles[h][:, t0 : t0 + 2, :])

        def store_words(h, count):
            nc.sync.dma_start(out=word_rows[:, head_cols(h, count)], in_=y_codes[:, head_cols(h, count)].bitcast(I32))

        def store_scales(h, count, queues):
            for n in range(QUADRANTS):
                queues[n % len(queues)].dma_start(
                    out=scale_rows[4 * n : 4 * n + 4, h * Q // 4 : (h + count) * Q // 4],
                    in_=y_scales[32 * n : 32 * n + 4, head_cols(h, count)].bitcast(I32),
                )

        load_attn_half(0, 0)
        nc.sync.dma_start(out=bias[:], in_=gate_bias.rearrange("(p t) h -> p (t h)", t=PACK))
        load_first_gates(slice(0, 1), slice(0, EARLY_QUERIES))
        load_attn_half(1, 0)
        load_values(0)
        load_attn_half(0, 1)
        load_attn_half(1, 1)
        load_values(1)
        load_values(2)
        load_values(3)
        load_attn_half(2, 0)
        load_attn_half(2, 1)
        load_first_gates(slice(0, 1), slice(EARLY_QUERIES, 2 * Q))
        load_first_gates(slice(1, PACK), slice(0, 2 * Q))
        load_attn(3)
        load_attn(4)
        load_gates(*LATER_GATE_LOADS[0])
        load_attn(5)
        load_gates(*LATER_GATE_LOADS[1])
        load_attn(6)
        load_attn(7)

        make_identity(nc, ident[:])
        gate_sigmoid(0, 0, slice(0, EARLY_QUERIES))

        turn_and_stage(0, 0, 0)
        turn_and_stage(0, 1, 1)
        turn_and_stage(1, 0, 2)
        turn_and_stage(1, 1, 3)
        group_values(0)
        quantize_attn(0, 0)
        quantize_values(0)
        quantize_attn(0, 1)
        turn_and_stage(0, 2, 0)
        turn_and_stage(0, 3, 1)
        group_values(1)
        turn_and_stage(1, 2, 2)
        quantize_values(1)
        multiply_first_pair(0)
        turn(1, 3, 3)
        multiply_first_pair(1)
        group_values(2)
        quantize_attn(0, 2)
        group_values(3)
        stage(1, 3, 3)
        quantize_values(2)
        quantize_values(3)
        quantize_attn(0, 3)
        for g in range(PASSES):
            turn_and_stage(2, g, g)
        quantize_attn(2, 0)
        quantize_attn(2, 2)
        multiply_first_pair(2)
        multiply_first_pair(3)
        for t in range(PACK):
            gate_sigmoid(0, t, slice(EARLY_QUERIES if t == 0 else 0, Q))
            gate_sigmoid(1, t)
            apply_gate(y_tiles[0][:, t, :], acc[t][:], sig[0][:, t * BANK : (t + 1) * BANK])
        sort_pairs(FIRST_SORTED_HEAD, 0)
        group_y(0)

        for h in range(2, LAST):
            next_is_last = h + 1 == LAST
            for g in range(PASSES):
                turn_and_stage(h + 1, g, g)
            for t in range(PACK):
                gate_sigmoid(h, t)
            if h == 2:
                sort_pairs(FIRST_SORTED_HEAD, 1)
                group_y(1)
                quantize_y(0)
            else:
                gate_bank(h - 1, 1)
                if not next_is_last:
                    sort_pairs(h + 2, 0)
                    sort_pairs(h + 2, 1)
                    group_y(h - 1)
            quantize_attn(h + 1, 0)
            if next_is_last:
                group_y(h - 1)
            quantize_attn(h + 1, 2)
            if next_is_last:
                quantize_y(h - 1)
            multiply_head(h)
            gate_bank(h, 0)
            if next_is_last:
                gate_bank(h, 1)
            else:
                quantize_y(h - 1)
            for first, count in Y_TILES:
                if first + count == h:
                    store_y(first, count)
            if h % 2 == 0:
                store_words(h - 2, 2)
        store_scales(0, LAST - 1, [nc.sync])
        store_y_slots(LAST - 1, 0)
        store_y_slots(LAST - 1, 2)

        for t in range(PACK):
            gate_sigmoid(LAST, t)
        for t in range(PACK):
            for g in range(PASSES):
                mx_pass(last_bank(t), t, g, LAST, 1)
            apply_gate(y_tiles[LAST][:, t, :], last_bank(t), sig_of(LAST)[:, t, :])
            if t % 2 == 1:
                store_y_slots(LAST, t - 1)
        group_y(LAST - 1)
        group_y(LAST)
        for h in (LAST - 1, LAST):
            quantize_y(h)
            store_words(h, 1)
        store_scales(LAST - 1, 2, [nc.scalar, nc.sync])
